import numpy as np
import ml_dtypes


def mxq(x, axis, fmt="e4m3"):
    dtype, down = {"e4m3": (ml_dtypes.float8_e4m3fn, 7), "e5m2": (ml_dtypes.float8_e5m2, 14)}[fmt]
    v = np.moveaxis(np.asarray(x, np.float32).astype(ml_dtypes.bfloat16).astype(np.float64), axis, -1)
    blocks = v.reshape(v.shape[:-1] + (-1, 32))
    amax = np.abs(blocks).max(-1, keepdims=True)
    byte = np.maximum(np.where(amax > 0, np.frexp(amax)[1] - 1 + 127, 0) - down, 1)
    scale = np.exp2(byte - 127.0)
    codes = (blocks / scale).astype(np.float32).astype(dtype).astype(np.float64)
    return np.moveaxis((codes * scale).reshape(v.shape), -1, axis)


WIDE = False


def mx_kscale(k):
    if not WIDE:
        return np.ones(k)
    levels = np.array([10, -10, 5, -5, 0])
    if k % 512:
        return np.exp2(np.random.permutation(np.resize(levels, k // 32))).repeat(32)
    a = np.empty((k // 512, 16))
    for p in range(k // 512):
        a[p, :8] = np.random.permutation(np.resize(levels, 8))
        for g in range(8):
            far = levels[np.abs(levels - a[p, g]) >= 10]
            a[p, g + 8] = far[np.random.randint(len(far))]
    return np.exp2(a.ravel()).repeat(32)


BF16 = ml_dtypes.bfloat16


def bf(x):
    return np.asarray(x, np.float32).astype(BF16)


def f64(x):
    return np.asarray(x).astype(np.float64)

E4M3FN = np.array([(-1.0 if i & 128 else 1.0) * ((1.0 + (i & 7) / 8.0) * 2.0 ** (((i >> 3) & 15) - 7) if i & 120 else (i & 7) * 2.0 ** -9) for i in range(256)])


def e4m3fn_bytes(y):
    return np.clip(np.asarray(y, np.float64), -448.0, 448.0).astype(np.float32).astype(ml_dtypes.float8_e4m3fn).view(np.uint8)


def e4m3fn_values(b):
    return E4M3FN[b]


T, D, F, N, B = 512, 1024, 2048, 1536, 128
FP8_MAX = 448.0


def setup_inputs():
    s, t = mx_kscale(D), mx_kscale(F)
    c = np.exp(0.5 * np.random.standard_normal(D))
    x = np.random.standard_normal((T, D)) * c * s
    w = np.random.standard_normal((N, D)) / np.sqrt(D) / s
    keys = np.random.standard_normal((D, F)) / np.sqrt(D) / s[:, None]
    values = np.random.standard_normal((F, N)) / np.sqrt(F) / t[:, None]
    g = (1 + 0.1 * np.random.standard_normal(F)) * t
    w_scale = (np.abs(w).reshape(N // B, B, D // B, B).max((1, 3)) / FP8_MAX).astype(np.float32)
    keys_scale = (np.abs(keys).max(1, keepdims=True) / FP8_MAX).astype(np.float32)
    values_scale = (np.abs(values).max(1, keepdims=True) / FP8_MAX).astype(np.float32)
    return {"x": bf(x), "c": bf(c), "g": bf(g),
            "w_bytes": e4m3fn_bytes(w / np.repeat(np.repeat(f64(w_scale), B, axis=0), B, axis=1)), "w_scale": w_scale,
            "keys_bytes": e4m3fn_bytes(keys / np.repeat(f64(keys_scale), F, axis=1)), "keys_scale": keys_scale,
            "values_bytes": e4m3fn_bytes(values / np.repeat(f64(values_scale), N, axis=1)), "values_scale": values_scale}


def reference(x, c, g, w_bytes, w_scale, keys_bytes, keys_scale, values_bytes, values_scale):
    w = e4m3fn_values(w_bytes) * np.repeat(np.repeat(f64(w_scale), B, axis=0), B, axis=1)
    keys = e4m3fn_values(keys_bytes) * np.repeat(f64(keys_scale), F, axis=1)
    values = e4m3fn_values(values_bytes) * np.repeat(f64(values_scale), N, axis=1)
    z = mxq(f64(x) / f64(c), 1, "e4m3")
    dense = z @ mxq(w, 1, "e4m3").T
    scores = z @ mxq(keys, 0, "e4m3")
    h = np.maximum(scores, 0.0) * f64(g)
    mix = mxq(h, 1, "e4m3") @ mxq(values, 0, "e4m3")
    return dense + mix

@@ -1,0 +1,509 @@
+from contextlib import ExitStack
+
+import concourse.mybir as mybir
+from concourse.masks import make_identity
+
+T, D, F, N = 512, 1024, 2048, 1536
+P = 128
+FLOPS = 2 * T * (D * N + D * F + F * N)
+
+F32 = mybir.dt.float32
+BF16 = mybir.dt.bfloat16
+U32 = mybir.dt.uint32
+U8 = mybir.dt.uint8
+FP8 = mybir.dt.float8_e4m3fn
+FP8X4 = mybir.dt.float8_e4m3fn_x4
+MULT = mybir.AluOpType.mult
+MAX = mybir.AluOpType.max
+COPY = mybir.ActivationFunctionType.Copy
+
+KG = D // 512
+FG = F // 512
+NC = N // 512
+TB = T // P
+
+ORDER = [('vw', ('k', 0, 0)), ('zt', 0), ('ww', 0, 0, 0), ('pe', ('k', 0, 0), 0), ('vw', ('k', 1, 0)), ('pe', ('k', 0, 0), 1), ('pc', ('k', 0, 0), 0), ('zs', 0, 0), ('zt', 1), ('pc', ('k', 0, 0), 1), ('ww', 0, 0, 1), ('pe', ('k', 1, 0), 0), ('zs', 1, 0), ('pe', ('k', 1, 0), 1), ('pc', ('k', 1, 0), 0), ('zs', 0, 1), ('wt', 0, 0), ('pc', ('k', 1, 0), 1), ('ww', 0, 1, 0), ('zs', 1, 1), ('wo', 0, 0), ('q', 'z', 0), ('q', 'z', 1), ('ww', 0, 1, 1), ('vw', ('k', 0, 1)), ('ww', 1, 0, 0), ('wt', 0, 1), ('q', ('k', 0, 0)), ('vw', ('k', 1, 1)), ('pe', ('k', 0, 1), 0), ('sw', ('v', 1, 0)), ('pe', ('k', 0, 1), 1), ('q', ('k', 1, 0)), ('pc', ('k', 0, 1), 0), ('vw', ('k', 0, 2)), ('sc', 0, 0), ('pc', ('k', 0, 1), 1), ('pe', ('k', 1, 1), 0), ('wo', 0, 1), ('q', ('k', 0, 1)), ('pe', ('k', 1, 1), 1), ('vw', ('k', 1, 2)), ('sc', 0, 1), ('pc', ('k', 1, 1), 0), ('pc', ('k', 1, 1), 1), ('pe', ('k', 0, 2), 0), ('gate', 0, 0), ('sw', ('v', 2, 0)), ('pe', ('k', 0, 2), 1), ('q', ('k', 1, 1)), ('sc', 0, 2), ('gate', 0, 1), ('pc', ('k', 0, 2), 0), ('vw', ('k', 0, 3)), ('sc', 0, 3), ('pc', ('k', 0, 2), 1), ('pe', ('k', 1, 2), 0), ('ww', 1, 0, 1), ('q', ('k', 0, 2)), ('pe', ('k', 1, 2), 1), ('gate', 0, 2), ('pc', ('k', 1, 2), 0), ('wt', 1, 0), ('gate', 0, 3), ('pc', ('k', 1, 2), 1), ('vw', ('k', 1, 3)), ('ww', 1, 1, 0), ('sc', 1, 0), ('q', 'h', 0), ('sc', 1, 1), ('wo', 1, 0), ('q', ('k', 1, 2)), ('pe', ('k', 0, 3), 0), ('gate', 1, 0), ('pe', ('k', 0, 3), 1), ('pc', ('k', 0, 3), 0), ('gate', 1, 1), ('sc', 1, 2), ('pc', ('k', 0, 3), 1), ('vw', ('v', 0, 0)), ('sc', 1, 3), ('ww', 1, 1, 1), ('pe', ('k', 1, 3), 0), ('q', ('k', 0, 3)), ('pe', ('k', 1, 3), 1), ('pc', ('k', 1, 3), 0), ('gate', 1, 2), ('wt', 1, 1), ('pc', ('k', 1, 3), 1), ('gate', 1, 3), ('sw', ('v', 3, 0)), ('il', ('v', 0, 0)), ('sc', 2, 0), ('sc', 2, 1), ('q', 'h', 1), ('vw', ('v', 1, 0)), ('wo', 1, 1), ('q', ('k', 1, 3)), ('gate', 2, 0), ('ww', 2, 0, 0), ('gate', 2, 1), ('sc', 2, 2), ('il', ('v', 1, 0)), ('sc', 2, 3), ('ww', 2, 0, 1), ('gate', 2, 2), ('sw', ('v', 0, 1)), ('wt', 2, 0), ('gate', 2, 3), ('q', 'w', 0, 0), ('sc', 3, 0), ('q', 'w', 1, 0), ('sc', 3, 1), ('gate', 3, 0), ('sw', ('v', 1, 1)), ('dense', 0), ('gate', 3, 1), ('q', 'h', 2), ('vw', ('v', 2, 0)), ('q', ('v', 0, 0)), ('sw', ('v', 2, 1)), ('sc', 3, 2), ('il', ('v', 2, 0)), ('sc', 3, 3), ('mix', 0, 0), ('gate', 3, 2), ('ww', 2, 1, 0), ('gate', 3, 3), ('q', ('v', 1, 0)), ('q', 'h', 3), ('wo', 2, 0), ('mix', 1, 0), ('q', 'w', 0, 1), ('ww', 2, 1, 1), ('q', 'w', 1, 1), ('il', ('v', 3, 0)), ('sw', ('v', 3, 1)), ('wt', 2, 1), ('q', ('v', 2, 0)), ('il', ('v', 0, 1)), ('mix', 2, 0), ('wo', 2, 1), ('q', ('v', 3, 0)), ('il', ('v', 1, 1)), ('mix', 3, 0), ('sw', ('v', 0, 2)), ('dense', 1), ('st', 0, 0), ('q', ('v', 0, 1)), ('st', 0, 1), ('il', ('v', 2, 1)), ('st', 0, 2), ('st', 0, 3), ('q', ('v', 1, 1)), ('sw', ('v', 1, 2)), ('mix', 0, 1), ('q', 'w', 0, 2), ('q', 'w', 1, 2), ('mix', 1, 1), ('sw', ('v', 2, 2)), ('il', ('v', 3, 1)), ('dense', 2), ('sw', ('v', 3, 2)), ('q', ('v', 2, 1)), ('il', ('v', 0, 2)), ('sw', ('v', 0, 3)), ('mix', 2, 1), ('q', ('v', 3, 1)), ('sw', ('v', 1, 3)), ('il', ('v', 1, 2)), ('mix', 3, 1), ('q', ('v', 0, 2)), ('il', ('v', 2, 2)), ('sw', ('v', 2, 3)), ('mix', 0, 2), ('q', ('v', 1, 2)), ('il', ('v', 3, 2)), ('mix', 1, 2), ('st', 1, 0), ('q', ('v', 2, 2)), ('st', 1, 1), ('il', ('v', 0, 3)), ('mix', 2, 2), ('st', 1, 2), ('q', ('v', 3, 2)), ('il', ('v', 1, 3)), ('st', 1, 3), ('mix', 3, 2), ('sw', ('v', 3, 3)), ('dense', 3), ('q', ('v', 0, 3)), ('il', ('v', 2, 3)), ('q', ('v', 1, 3)), ('st', 2, 0), ('mix', 0, 3), ('il', ('v', 3, 3)), ('st', 2, 1), ('st', 2, 2), ('mix', 1, 3), ('st', 2, 3), ('q', ('v', 2, 3)), ('q', ('v', 3, 3)), ('mix', 2, 3), ('mix', 3, 3), ('st', 3, 0), ('st', 3, 1), ('st', 3, 2), ('st', 3, 3)]
+KEYS_VEC = 4
+VAL_VEC = [4, 2, 2, 0, 0, 0, 0, 0, 0, 0, 0, 0, 0, 0, 0, 0]
+VAL_PE = []
+KEYS_PE = 8
+TURN = 2
+PLB = 8
+W_RATE = [2, 3, 4, 5, 6, 7, 8, 9, 10, 11, 12] + [12] * 13
+ST_LAG = 7
+GATE_LAG = 3
+SC = 2
+CH = [(0, 512), (512, 512), (1024, 256), (1280, 256)]
+
+
+def tile_smoothed_linear_slot_memory_d5_kernel(
+    tc, x, c, g, w_bytes, w_scale, keys_bytes, keys_scale, values_bytes, values_scale, out
+):
+    nc = tc.nc
+    with ExitStack() as ctx:
+        keep = ctx.enter_context(tc.tile_pool(name="keep", bufs=1))
+        stage = ctx.enter_context(tc.tile_pool(name="stage", bufs=4))
+        psum = ctx.enter_context(tc.psum_pool(name="psum", bufs=1))
+        ctx.enter_context(tc.manual_schedule())
+
+        ks = keep.tile([P, KG, 4], F32, name="ks")
+        nc.sync.dma_start(out=ks[:], in_=keys_scale.rearrange("(g p t) o -> p g (t o)", p=P, t=4))
+        c_sb = keep.tile([P, KG, 1, 2, 2], BF16, name="c_sb")
+        nc.scalar.dma_start(
+            out=c_sb[:].rearrange("p g o u e -> p g (o u e)"), in_=c.rearrange("(g p t) -> p g t", p=P, t=4)
+        )
+        ident = keep.tile([P, P], F32, name="ident")
+        make_identity(nc, ident[:])
+        ident_bf = keep.tile([P, P], BF16, name="ident_bf")
+        nc.vector.tensor_copy(out=ident_bf[:], in_=ident[:])
+        g_sb = keep.tile([P, FG, 1, 4], BF16, name="g_sb")
+        nc.gpsimd.dma_start(
+            out=g_sb[:].rearrange("p g o t -> p g (o t)"), in_=g.rearrange("(g p t) -> p g t", p=P, t=4)
+        )
+        ws = keep.tile([P, 96], F32, name="ws")
+        nc.gpsimd.dma_start(out=ws[:], in_=w_scale.rearrange("a b -> (a b)").partition_broadcast(P))
+        vs = keep.tile([P, FG, 4], F32, name="vs")
+        nc.gpsimd.dma_start(out=vs[:], in_=values_scale.rearrange("(g p t) o -> p g (t o)", p=P, t=4))
+
+        key_rows = keys_bytes.rearrange("(g p t) n -> g p t n", p=P, t=4)
+        val_rows = values_bytes.rearrange("(g p t) n -> g p t n", p=P, t=4)
+        w_rows = w_bytes.rearrange("(b p) k -> p b k", p=P)
+        x_rows = x.rearrange("(i p) k -> p i k", p=P)
+
+        kraw, vraw, wraw, xt = {}, {}, {}, {}
+
+        def load_keys(gi, lo, width):
+            raw = keep.tile([P, 4, width], U8, name="kraw%d_%d" % (gi, lo))
+            nc.sync.dma_start(out=raw[:], in_=key_rows[gi][:, :, lo : lo + width])
+            for f0 in range(lo, lo + width, 512):
+                kraw[gi, f0 // 512] = (raw, f0 - lo)
+
+        def load_x(h):
+            xs = keep.tile([P, 2, D], BF16, name="x%d" % h)
+            nc.sync.dma_start(out=xs[:], in_=x_rows[:, 2 * h : 2 * h + 2, :])
+            xt[h] = xs
+
+        def load_w(ci, h):
+            raw = keep.tile([P, 2, D], U8, name="wraw%d_%d" % (ci, h))
+            nc.sync.dma_start(out=raw[:], in_=w_rows[:, 4 * ci + 2 * h : 4 * ci + 2 * h + 2, :])
+            wraw[ci, h] = raw
+
+        load_keys(0, 0, 512)
+        load_x(0)
+        load_w(0, 0)
+        load_keys(1, 0, 512)
+        load_x(1)
+        load_w(0, 1)
+        load_keys(0, 512, 512)
+        load_keys(1, 512, 512)
+        load_w(1, 0)
+        load_keys(0, 1024, 1024)
+        load_w(1, 1)
+        load_keys(1, 1024, 1024)
+        load_w(2, 0)
+        load_w(2, 1)
+        for ci in range(NC):
+            for gi in range(FG):
+                raw = keep.tile([P, 4, 512], U8, name="vraw%d_%d" % (gi, ci))
+                nc.sync.dma_start(out=raw[:], in_=val_rows[gi][:, :, 512 * ci : 512 * ci + 512])
+                vraw[gi, ci] = raw
+
+        rc = keep.tile([P, KG, 1, 2, 2], F32, name="rc")
+        nc.vector.reciprocal(out=rc[:], in_=c_sb[:])
+
+        def operand(name, width=512):
+            return (
+                keep.tile([P, width], U32, name=name + "_q", align_bytes=64),
+                keep.tile([P, width], U8, name=name + "_s", align_bytes=64),
+            )
+
+        zq = [operand("z%d" % gi) for gi in range(KG)]
+        kq = {(gi, fi): operand("k%d_%d" % (gi, fi)) for gi in range(KG) for fi in range(FG)}
+        wq = {(gi, ci): operand("w%d_%d" % (gi, ci)) for gi in range(KG) for ci in range(NC)}
+        hq = [operand("h%d" % gi) for gi in range(FG)]
+        vq = {(gi, ci): operand("v%d_%d" % (gi, ci), CH[ci][1]) for gi in range(FG) for ci in range(len(CH))}
+
+        def quantize(dst, src):
+            nc.vector.quantize_mx(
+                out=dst[0][:].bitcast(FP8X4), scales=dst[1][:], in_=src[:].rearrange("p n j -> p (n j)")
+            )
+
+        def grouped_tile(name, bufs, width=512):
+            return stage.tile([P, width, 4], BF16, name=name, bufs=bufs, align_bytes=64)
+
+        def mm(o, a, a_lo, b, b_lo, width, start, stop):
+            nc.tensor.matmul_mx(
+                out=o,
+                lhsT=a[0][:, a_lo : a_lo + P].bitcast(FP8X4),
+                lhsT_scale=a[1][:, a_lo : a_lo + P],
+                rhs=b[0][:, b_lo : b_lo + width].bitcast(FP8X4),
+                rhs_scale=b[1][:, b_lo : b_lo + width],
+                start=start,
+                stop=stop,
+            )
+
+        zg = [grouped_tile("wg%d" % gi, 2) for gi in range(KG)]
+
+        def z_turn(gi, h):
+            bank = psum.tile([P, 2, 256], F32, name="o%d" % (2 * h + gi), bufs=1)
+            for i in range(2):
+                words = xt[h][:, i, :].bitcast(F32)
+                for u in range(2):
+                    nc.tensor.transpose(
+                        bank[:, u, P * i : P * i + P], words[:, 256 * gi + u : 256 * (gi + 1) : 2], ident[:]
+                    )
+            return bank
+
+        def z_scale(gi, h, bank):
+            nc.vector.tensor_tensor(
+                out=zg[gi][:, 256 * h : 256 * h + 256, :].rearrange("p r (u e) -> p r u e", u=2),
+                in0=bank[:].rearrange("p u r -> p (u r)").bitcast(BF16).rearrange("p (u r e) -> p r u e", u=2, e=2),
+                in1=rc[:, gi].to_broadcast([P, 256, 2, 2]),
+                op=MULT,
+            )
+
+        jobs, lists = {}, {"V": [], "S": [], "T": []}
+
+        def job(engine, key, deps, fn):
+            jobs[key] = (engine, deps, fn)
+            lists[engine].append(key)
+
+        done, cursor, active = set(), {"V": 0, "S": 0, "T": 0}, []
+
+        def emit(key):
+            if key in done:
+                return
+            engine = jobs[key][0]
+            while key not in done:
+                k = lists[engine][cursor[engine]]
+                assert k not in active, (k, active)
+                active.append(k)
+                for d in jobs[k][1]:
+                    emit(d)
+                active.pop()
+                if k in done:
+                    continue
+                cursor[engine] += 1
+                done.add(k)
+                jobs[k][2]()
+
+        planes, grouped, banks, wb, obank = {}, {}, {}, {}, {}
+
+        def get(d, key, make):
+            if key not in d:
+                d[key] = make()
+            return d[key]
+
+        def source(key):
+            kind, gi, ni = key
+            if kind == "k":
+                raw, lo = kraw[gi, ni]
+                return raw, lo, ks[:, gi, :]
+            return vraw[gi, CH[ni][0] // 512], CH[ni][0] % 512, vs[:, gi, :]
+
+        def width_of(key):
+            return 512 if key[0] == "k" else CH[key[2]][1]
+
+        def widen(key, js, vec):
+            raw, lo, scale = source(key)
+            w = width_of(key)
+            pl = get(planes, key, lambda: stage.tile([P, 4, w], BF16, name="planes", bufs=PLB))
+            for j in js:
+                src = raw[:, j, lo : lo + w].bitcast(FP8)
+                if vec:
+                    nc.vector.tensor_scalar(
+                        out=pl[:, j, :], in0=src, scalar1=scale[:, j : j + 1], scalar2=None, op0=MULT
+                    )
+                else:
+                    nc.scalar.activation(out=pl[:, j, :], in_=src, func=COPY, scale=scale[:, j : j + 1])
+
+        def interleave(key):
+            gr = get(grouped, key, lambda: grouped_tile("gr", 3, width_of(key)))
+            pl = planes.pop(key)
+            if key[0] == "k":
+                nc.vector.tensor_copy(
+                    out=gr[:].rearrange("p (t m) j -> p t m j", t=4), in_=pl[:].rearrange("p j (m t) -> p t m j", t=4)
+                )
+            else:
+                nc.vector.tensor_copy(
+                    out=gr[:].rearrange("p (n i) j -> p n j i", i=4), in_=pl[:].rearrange("p j (n i) -> p n j i", i=4)
+                )
+
+        def pe_interleave(key, half):
+            pl = planes[key]
+            bank = psum.tile([P, 1024], BF16, name="turn", bufs=TURN)
+            for q in range(2):
+                t = 2 * half + q
+                if key[0] == "k":
+                    rhs = pl[:].rearrange("p j (m t) -> p t m j", t=4)[:, t]
+                else:
+                    rhs = pl[:, :, P * t : P * t + P].rearrange("p j n -> p n j")
+                nc.tensor.matmul(
+                    out=bank[:, 512 * q : 512 * q + 512].rearrange("p (n j) -> p n j", j=4),
+                    lhsT=ident_bf[:],
+                    rhs=rhs,
+                    start=True,
+                    stop=True,
+                )
+            banks[key, half] = bank
+            if half == 1:
+                planes.pop(key)
+
+        def pe_copy(key, half):
+            gr = get(grouped, key, lambda: grouped_tile("gr", 3))
+            nc.scalar.copy(
+                out=gr[:, 256 * half : 256 * half + 256, :].rearrange("p n j -> p (n j)"), in_=banks.pop((key, half))[:]
+            )
+
+        def w_widen(ci, h, i):
+            t = get(wb, (ci, h), lambda: stage.tile([P, 2, D], BF16, name="wb", bufs=2))
+            b = 4 * ci + 2 * h + i
+            for q in range(8):
+                nc.scalar.activation(
+                    out=t[:, i, P * q : P * q + P],
+                    in_=wraw[ci, h][:, i, P * q : P * q + P].bitcast(FP8),
+                    func=COPY,
+                    scale=ws[:, 8 * b + q : 8 * b + q + 1],
+                )
+
+        def w_turn(ci, h):
+            for gi in range(KG):
+                if ci < 2:
+                    bank = psum.tile([P, 2, 256], F32, name="o%d" % (2 * h + gi), bufs=1)
+                else:
+                    bank = psum.tile([P, 2, 256], F32, name="turn", bufs=TURN)
+                for i in range(2):
+                    words = wb[ci, h][:, i, :].bitcast(F32)
+                    for u in range(2):
+                        nc.tensor.transpose(
+                            bank[:, u, P * i : P * i + P], words[:, 256 * gi + u : 256 * (gi + 1) : 2], ident[:]
+                        )
+                banks["w", ci, h, gi] = bank
+
+        def w_out(ci, h):
+            for gi in range(KG):
+                gr = get(grouped, ("w", gi, ci), lambda: grouped_tile("wg%d" % gi, 2))
+                dst = gr[:].rearrange("p n j -> p (n j)").bitcast(F32)
+                nc.scalar.copy(
+                    out=dst[:, 512 * h : 512 * h + 512].rearrange("p (n u) -> p n u", u=2),
+                    in_=banks.pop(("w", ci, h, gi))[:].rearrange("p u n -> p n u"),
+                )
+
+        def z_turns(h):
+            for gi in range(KG):
+                banks["z", gi, h] = z_turn(gi, h)
+
+        def scores(fi, i):
+            bank = psum.tile([P, 4, P], F32, name="sc", bufs=SC)
+            for t in range(4):
+                for gi in range(KG):
+                    mm(bank[:, t, :], kq[gi, fi], P * t, zq[gi], P * i, P, gi == 0, gi == KG - 1)
+            banks["s", fi, i] = bank
+
+        def gate(fi, i):
+            gr = get(grouped, ("h", fi), lambda: grouped_tile("hg", 2))
+            nc.vector.scalar_tensor_tensor(
+                out=gr[:, P * i : P * i + P, :],
+                in0=banks.pop(("s", fi, i))[:].rearrange("p t n -> p n t"),
+                scalar=0.0,
+                in1=g_sb[:, fi].to_broadcast([P, P, 4]),
+                op0=MAX,
+                op1=MULT,
+            )
+
+        def dense(ci):
+            lo, width = CH[ci]
+            for i in range(TB):
+                if ci % 2 == 0:
+                    obank[ci, i] = psum.tile([P, width], F32, name="o%d" % i, bufs=1)
+                elif i < 2:
+                    obank[ci, i] = psum.tile([P, width], F32, name="sc", bufs=SC)
+                else:
+                    obank[ci, i] = psum.tile([P, width], F32, name="turn", bufs=TURN)
+            for gi in range(KG):
+                for i in range(TB):
+                    mm(obank[ci, i][:], zq[gi], P * i, wq[gi, lo // 512], lo % 512, width, gi == 0, False)
+
+        def mix(gi, ci):
+            for i in range(TB):
+                mm(obank[ci, i][:], hq[gi], P * i, vq[gi, ci], 0, CH[ci][1], False, gi == FG - 1)
+
+        def store(ci, i, vec):
+            lo, width = CH[ci]
+            res = stage.tile([P, width], F32, name="res", bufs=8)
+            if vec:
+                nc.vector.tensor_copy(out=res[:], in_=obank[ci, i][:])
+            else:
+                nc.scalar.copy(out=res[:], in_=obank[ci, i][:])
+            nc.sync.dma_start(out=out[P * i : P * i + P, lo : lo + width], in_=res[:])
+
+        keys = [("k", gi, fi) for fi in range(FG) for gi in range(KG)]
+        vals = [("v", gi, ci) for ci in range(len(CH)) for gi in range(FG)]
+        vec_planes = {k: KEYS_VEC for k in keys}
+        vec_planes.update(zip(vals, VAL_VEC))
+        by_pe = set(keys[:KEYS_PE]) | {vals[n] for n in VAL_PE}
+        for k in keys + vals:
+            if k in by_pe and k not in vals:
+                pass
+
+        def v_widen(k):
+            if vec_planes[k]:
+                job("V", ("vw", k), [], lambda: widen(k, range(vec_planes[k]), True))
+
+        def widened(k):
+            return ([("vw", k)] if vec_planes[k] else []) + ([("sw", k)] if vec_planes[k] < 4 else [])
+
+        def v_inter(k):
+            if k not in by_pe:
+                job("V", ("il", k), widened(k), lambda: interleave(k))
+
+        def v_quant(k):
+            dst = kq[k[1:]] if k[0] == "k" else vq[k[1:]]
+            deps = [("pc", k, 0), ("pc", k, 1)] if k in by_pe else [("il", k)]
+            job("V", ("q", k), deps, lambda: quantize(dst, grouped[k]))
+
+        def v_wquant(ci):
+            for gi in range(KG):
+                job(
+                    "V",
+                    ("q", "w", gi, ci),
+                    [("wo", ci, 0), ("wo", ci, 1)],
+                    lambda gi=gi: quantize(wq[gi, ci], grouped["w", gi, ci]),
+                )
+
+        def v_gates(fi, blocks):
+            for i in blocks:
+                job("V", ("gate", fi, i), [("sc", fi, i)], lambda i=i: gate(fi, i))
+
+        def v_hquant(fi):
+            job("V", ("q", "h", fi), [("gate", fi, i) for i in range(TB)], lambda: quantize(hq[fi], grouped["h", fi]))
+
+        def v_z(h):
+            for gi in range(KG):
+                job("V", ("zs", gi, h), [("zt", h)], lambda gi=gi: z_scale(gi, h, banks.pop(("z", gi, h))))
+
+        v_widen(keys[0])
+        v_z(0)
+        v_widen(keys[1])
+        v_inter(keys[0])
+        v_z(1)
+        for gi in range(KG):
+            job("V", ("q", "z", gi), [("zs", gi, 0), ("zs", gi, 1)], lambda gi=gi: quantize(zq[gi], zg[gi]))
+        v_inter(keys[1])
+        for r, k in enumerate(keys):
+            ahead = (keys + vals)[r + 2]
+            v_widen(ahead)
+            v_quant(k)
+            if r >= GATE_LAG:
+                s = r - GATE_LAG
+                v_gates(s // 2, (0, 1) if s % 2 == 0 else (2, 3))
+            v_inter(ahead)
+            if r > GATE_LAG and (r - GATE_LAG) % 2 == 1:
+                v_hquant((r - GATE_LAG) // 2)
+        for s in range(8 - GATE_LAG, 8):
+            v_gates(s // 2, (0, 1) if s % 2 == 0 else (2, 3))
+            if s == 8 - GATE_LAG:
+                v_wquant(0)
+            if s == 6:
+                v_hquant(2)
+        for n, k in enumerate(vals):
+            if n + 2 < len(vals):
+                v_widen(vals[n + 2])
+            if n + 1 < len(vals) and n > 0:
+                v_inter(vals[n + 1])
+            if n == 0:
+                v_hquant(3)
+            v_quant(k)
+            if n == 1:
+                v_wquant(1)
+            if n == 5:
+                v_wquant(2)
+
+        halves = [(ci, h) for ci in range(NC) for h in range(2)]
+
+        def s_widen(k):
+            if vec_planes[k] < 4:
+                job("S", ("sw", k), [], lambda: widen(k, range(vec_planes[k], 4), False))
+
+        def s_copy(k):
+            for half in range(2):
+                if k in by_pe:
+                    job("S", ("pc", k, half), [("pe", k, half)], lambda half=half: pe_copy(k, half))
+
+        def s_w(n, i):
+            if n < len(halves):
+                job("S", ("ww",) + halves[n] + (i,), [], lambda: w_widen(*halves[n], i))
+
+        def s_wout(n):
+            if 0 <= n < len(halves):
+                job("S", ("wo",) + halves[n], [("wt",) + halves[n]], lambda: w_out(*halves[n]))
+
+        tiles = [(n, i) for n in range(len(halves)) for i in range(2)]
+        w_next = [0]
+
+        def s_wtiles(upto):
+            while w_next[0] < min(upto, 12):
+                n, i = tiles[w_next[0]]
+                s_w(n, i)
+                w_next[0] += 1
+                if i == 0:
+                    s_wout(n - 1)
+                if w_next[0] == 12:
+                    s_wout(n)
+
+        for r, k in enumerate(keys):
+            s_widen(k)
+            s_copy(k)
+            s_wtiles(W_RATE[r])
+        for n in range(len(vals)):
+            if n < len(vals):
+                s_widen(vals[n])
+                s_copy(vals[n])
+                s_wtiles(W_RATE[8 + n])
+            ci = (n - ST_LAG) // 4
+            if (n - ST_LAG) % 4 == 0 and 0 <= ci < 3:
+                for i in range(TB):
+                    job("S", ("st", ci, i), [("mix", 3, ci)], lambda ci=ci, i=i: store(ci, i, False))
+        last = len(CH) - 1
+        for ci in range(1, last + 1):
+            for i in range(TB):
+                if ("st", ci, i) not in jobs:
+                    e = "V" if ci == last and i % 2 else "S"
+                    job(e, ("st", ci, i), [("mix", 3, ci)], lambda ci=ci, i=i, e=e: store(ci, i, e == "V"))
+
+        def t_pe(k):
+            for half in range(2):
+                if k in by_pe:
+                    job("T", ("pe", k, half), widened(k), lambda half=half: pe_interleave(k, half))
+
+        def t_scores(fi):
+            for i in range(TB):
+                job("T", ("sc", fi, i), [("q", ("k", gi, fi)) for gi in range(KG)] + [("q", "z", gi) for gi in range(KG)], lambda i=i: scores(fi, i))
+
+        def t_zturn(h):
+            job("T", ("zt", h), [], lambda: z_turns(h))
+
+        def t_wturn(n):
+            if 0 <= n < len(halves):
+                job("T", ("wt",) + halves[n], [("ww",) + halves[n] + (i,) for i in range(2)], lambda: w_turn(*halves[n]))
+
+        t_zturn(0)
+        t_pe(keys[0])
+        t_zturn(1)
+        t_wturn(0)
+        t_pe(keys[1])
+        for r, k in enumerate(keys):
+            if r + 2 < len(keys):
+                t_pe(keys[r + 2])
+            if r % 2 == 1:
+                t_scores(r // 2)
+            t_wturn(r + 1)
+        for ci in range(len(CH)):
+            job("T", ("dense", ci), [("q", "w", gi, min(ci, 2)) for gi in range(KG)] + [("st", ci - 2, i) for i in range(TB) if ci > 1] + ([("wt", 2, 1), ("gate", 3, 3)] if ci == 1 else []), lambda ci=ci: dense(ci))
+            for gi in range(FG):
+                if 4 * ci + gi + 1 < len(vals):
+                    t_pe(vals[4 * ci + gi + 1])
+                job("T", ("mix", gi, ci), [("q", "h", gi), ("q", ("v", gi, ci)), ("mix", gi - 1, ci) if gi else ("dense", ci)], lambda gi=gi, ci=ci: mix(gi, ci))
+
+        for key in ORDER:
+            jobs[key][2]()

@@ -22,11 +22,11 @@ FG = F // 512
 NC = N // 512
 TB = T // P
 
-ORDER = [('vw', ('k', 0, 0)), ('zt', 0), ('ww', 0, 0, 0), ('pe', ('k', 0, 0), 0), ('vw', ('k', 1, 0)), ('pe', ('k', 0, 0), 1), ('pc', ('k', 0, 0), 0), ('zs', 0, 0), ('zt', 1), ('pc', ('k', 0, 0), 1), ('ww', 0, 0, 1), ('pe', ('k', 1, 0), 0), ('zs', 1, 0), ('pe', ('k', 1, 0), 1), ('pc', ('k', 1, 0), 0), ('zs', 0, 1), ('wt', 0, 0), ('pc', ('k', 1, 0), 1), ('ww', 0, 1, 0), ('zs', 1, 1), ('wo', 0, 0), ('q', 'z', 0), ('q', 'z', 1), ('ww', 0, 1, 1), ('vw', ('k', 0, 1)), ('ww', 1, 0, 0), ('wt', 0, 1), ('q', ('k', 0, 0)), ('vw', ('k', 1, 1)), ('pe', ('k', 0, 1), 0), ('sw', ('v', 1, 0)), ('pe', ('k', 0, 1), 1), ('q', ('k', 1, 0)), ('pc', ('k', 0, 1), 0), ('vw', ('k', 0, 2)), ('sc', 0, 0), ('pc', ('k', 0, 1), 1), ('pe', ('k', 1, 1), 0), ('wo', 0, 1), ('q', ('k', 0, 1)), ('pe', ('k', 1, 1), 1), ('vw', ('k', 1, 2)), ('sc', 0, 1), ('pc', ('k', 1, 1), 0), ('pc', ('k', 1, 1), 1), ('pe', ('k', 0, 2), 0), ('gate', 0, 0), ('sw', ('v', 2, 0)), ('pe', ('k', 0, 2), 1), ('q', ('k', 1, 1)), ('sc', 0, 2), ('gate', 0, 1), ('pc', ('k', 0, 2), 0), ('vw', ('k', 0, 3)), ('sc', 0, 3), ('pc', ('k', 0, 2), 1), ('pe', ('k', 1, 2), 0), ('ww', 1, 0, 1), ('q', ('k', 0, 2)), ('pe', ('k', 1, 2), 1), ('gate', 0, 2), ('pc', ('k', 1, 2), 0), ('wt', 1, 0), ('gate', 0, 3), ('pc', ('k', 1, 2), 1), ('vw', ('k', 1, 3)), ('ww', 1, 1, 0), ('sc', 1, 0), ('q', 'h', 0), ('sc', 1, 1), ('wo', 1, 0), ('q', ('k', 1, 2)), ('pe', ('k', 0, 3), 0), ('gate', 1, 0), ('pe', ('k', 0, 3), 1), ('pc', ('k', 0, 3), 0), ('gate', 1, 1), ('sc', 1, 2), ('pc', ('k', 0, 3), 1), ('vw', ('v', 0, 0)), ('sc', 1, 3), ('ww', 1, 1, 1), ('pe', ('k', 1, 3), 0), ('q', ('k', 0, 3)), ('pe', ('k', 1, 3), 1), ('pc', ('k', 1, 3), 0), ('gate', 1, 2), ('wt', 1, 1), ('pc', ('k', 1, 3), 1), ('gate', 1, 3), ('sw', ('v', 3, 0)), ('il', ('v', 0, 0)), ('sc', 2, 0), ('sc', 2, 1), ('q', 'h', 1), ('vw', ('v', 1, 0)), ('wo', 1, 1), ('q', ('k', 1, 3)), ('gate', 2, 0), ('ww', 2, 0, 0), ('gate', 2, 1), ('sc', 2, 2), ('il', ('v', 1, 0)), ('sc', 2, 3), ('ww', 2, 0, 1), ('gate', 2, 2), ('sw', ('v', 0, 1)), ('wt', 2, 0), ('gate', 2, 3), ('q', 'w', 0, 0), ('sc', 3, 0), ('q', 'w', 1, 0), ('sc', 3, 1), ('gate', 3, 0), ('sw', ('v', 1, 1)), ('dense', 0), ('gate', 3, 1), ('q', 'h', 2), ('vw', ('v', 2, 0)), ('q', ('v', 0, 0)), ('sw', ('v', 2, 1)), ('sc', 3, 2), ('il', ('v', 2, 0)), ('sc', 3, 3), ('mix', 0, 0), ('gate', 3, 2), ('ww', 2, 1, 0), ('gate', 3, 3), ('q', ('v', 1, 0)), ('q', 'h', 3), ('wo', 2, 0), ('mix', 1, 0), ('q', 'w', 0, 1), ('ww', 2, 1, 1), ('q', 'w', 1, 1), ('il', ('v', 3, 0)), ('sw', ('v', 3, 1)), ('wt', 2, 1), ('q', ('v', 2, 0)), ('il', ('v', 0, 1)), ('mix', 2, 0), ('wo', 2, 1), ('q', ('v', 3, 0)), ('il', ('v', 1, 1)), ('mix', 3, 0), ('sw', ('v', 0, 2)), ('dense', 1), ('st', 0, 0), ('q', ('v', 0, 1)), ('st', 0, 1), ('il', ('v', 2, 1)), ('st', 0, 2), ('st', 0, 3), ('q', ('v', 1, 1)), ('sw', ('v', 1, 2)), ('mix', 0, 1), ('q', 'w', 0, 2), ('q', 'w', 1, 2), ('mix', 1, 1), ('sw', ('v', 2, 2)), ('il', ('v', 3, 1)), ('dense', 2), ('sw', ('v', 3, 2)), ('q', ('v', 2, 1)), ('il', ('v', 0, 2)), ('sw', ('v', 0, 3)), ('mix', 2, 1), ('q', ('v', 3, 1)), ('sw', ('v', 1, 3)), ('il', ('v', 1, 2)), ('mix', 3, 1), ('q', ('v', 0, 2)), ('il', ('v', 2, 2)), ('sw', ('v', 2, 3)), ('mix', 0, 2), ('q', ('v', 1, 2)), ('il', ('v', 3, 2)), ('mix', 1, 2), ('st', 1, 0), ('q', ('v', 2, 2)), ('st', 1, 1), ('il', ('v', 0, 3)), ('mix', 2, 2), ('st', 1, 2), ('q', ('v', 3, 2)), ('il', ('v', 1, 3)), ('st', 1, 3), ('mix', 3, 2), ('sw', ('v', 3, 3)), ('dense', 3), ('q', ('v', 0, 3)), ('il', ('v', 2, 3)), ('q', ('v', 1, 3)), ('st', 2, 0), ('mix', 0, 3), ('il', ('v', 3, 3)), ('st', 2, 1), ('st', 2, 2), ('mix', 1, 3), ('st', 2, 3), ('q', ('v', 2, 3)), ('q', ('v', 3, 3)), ('mix', 2, 3), ('mix', 3, 3), ('st', 3, 0), ('st', 3, 1), ('st', 3, 2), ('st', 3, 3)]
-KEYS_VEC = 4
-VAL_VEC = [4, 2, 2, 0, 0, 0, 0, 0, 0, 0, 0, 0, 0, 0, 0, 0]
+ORDER = [('sw', ('k', 0, 0)), ('vw', ('k', 0, 0)), ('zt', 0), ('il', ('k', 0, 0)), ('ww', 0, 0, 0), ('zs', 0, 0), ('sw', ('k', 1, 0)), ('zt', 1), ('zs', 1, 0), ('ww', 0, 0, 1), ('vw', ('k', 1, 0)), ('sw', ('k', 0, 1)), ('zs', 0, 1), ('wt', 0, 0), ('zs', 1, 1), ('sw', ('k', 1, 1)), ('q', 'z', 0), ('q', 'z', 1), ('sw', ('k', 0, 2)), ('il', ('k', 1, 0)), ('vw', ('k', 0, 1)), ('q', ('k', 0, 0)), ('il', ('k', 0, 1)), ('sw', ('k', 1, 2)), ('vw', ('k', 1, 1)), ('q', ('k', 1, 0)), ('il', ('k', 1, 1)), ('sw', ('k', 0, 3)), ('sc', 0, 0), ('sc', 0, 1), ('q', ('k', 0, 1)), ('il', ('k', 0, 2)), ('sw', ('k', 1, 3)), ('q', ('k', 1, 1)), ('gate', 0, 0), ('gate', 0, 1), ('sc', 0, 2), ('ww', 0, 1, 0), ('il', ('k', 1, 2)), ('sc', 0, 3), ('wo', 0, 0), ('q', ('k', 0, 2)), ('gate', 0, 2), ('ww', 0, 1, 1), ('gate', 0, 3), ('sc', 1, 0), ('il', ('k', 0, 3)), ('sc', 1, 1), ('sw', ('v', 2, 0)), ('wt', 0, 1), ('ww', 1, 0, 0), ('q', 'h', 0), ('q', ('k', 1, 2)), ('gate', 1, 0), ('wo', 0, 1), ('gate', 1, 1), ('sc', 1, 2), ('il', ('k', 1, 3)), ('ww', 1, 0, 1), ('sc', 1, 3), ('ww', 1, 1, 0), ('vw', ('v', 0, 0)), ('wt', 1, 0), ('q', ('k', 0, 3)), ('ww', 1, 1, 1), ('gate', 1, 2), ('gate', 1, 3), ('sc', 2, 0), ('wo', 1, 0), ('il', ('v', 0, 0)), ('sc', 2, 1), ('sw', ('v', 3, 0)), ('wt', 1, 1), ('q', 'h', 1), ('vw', ('v', 1, 0)), ('wo', 1, 1), ('q', ('k', 1, 3)), ('gate', 2, 0), ('sw', ('v', 0, 1)), ('gate', 2, 1), ('sc', 2, 2), ('il', ('v', 1, 0)), ('sc', 2, 3), ('gate', 2, 2), ('sw', ('v', 1, 1)), ('gate', 2, 3), ('sc', 3, 0), ('q', 'w', 0, 0), ('sc', 3, 1), ('q', 'w', 1, 0), ('gate', 3, 0), ('dense', 0), ('sw', ('v', 2, 1)), ('gate', 3, 1), ('q', 'h', 2), ('vw', ('v', 2, 0)), ('q', ('v', 0, 0)), ('sc', 3, 2), ('ww', 2, 0, 0), ('il', ('v', 2, 0)), ('sc', 3, 3), ('mix', 0, 0), ('ww', 2, 0, 1), ('gate', 3, 2), ('gate', 3, 3), ('ww', 2, 1, 0), ('wt', 2, 0), ('q', ('v', 1, 0)), ('q', 'h', 3), ('mix', 1, 0), ('wo', 2, 0), ('q', 'w', 0, 1), ('q', 'w', 1, 1), ('ww', 2, 1, 1), ('il', ('v', 3, 0)), ('sw', ('v', 3, 1)), ('wt', 2, 1), ('q', ('v', 2, 0)), ('il', ('v', 0, 1)), ('mix', 2, 0), ('wo', 2, 1), ('q', ('v', 3, 0)), ('il', ('v', 1, 1)), ('mix', 3, 0), ('sw', ('v', 0, 2)), ('dense', 1), ('q', ('v', 0, 1)), ('st', 0, 0), ('il', ('v', 2, 1)), ('st', 0, 1), ('st', 0, 2), ('st', 0, 3), ('q', ('v', 1, 1)), ('mix', 0, 1), ('sw', ('v', 1, 2)), ('q', 'w', 0, 2), ('q', 'w', 1, 2), ('mix', 1, 1), ('sw', ('v', 2, 2)), ('il', ('v', 3, 1)), ('dense', 2), ('sw', ('v', 3, 2)), ('q', ('v', 2, 1)), ('il', ('v', 0, 2)), ('mix', 2, 1), ('sw', ('v', 0, 3)), ('q', ('v', 3, 1)), ('il', ('v', 1, 2)), ('mix', 3, 1), ('sw', ('v', 1, 3)), ('q', ('v', 0, 2)), ('il', ('v', 2, 2)), ('mix', 0, 2), ('st', 1, 0), ('q', ('v', 1, 2)), ('st', 1, 1), ('il', ('v', 3, 2)), ('mix', 1, 2), ('st', 1, 2), ('q', ('v', 2, 2)), ('il', ('v', 0, 3)), ('st', 1, 3), ('mix', 2, 2), ('sw', ('v', 2, 3)), ('q', ('v', 3, 2)), ('dense', 3), ('il', ('v', 1, 3)), ('q', ('v', 0, 3)), ('sw', ('v', 3, 3)), ('mix', 3, 2), ('il', ('v', 2, 3)), ('mix', 0, 3), ('q', ('v', 1, 3)), ('q', ('v', 2, 3)), ('st', 2, 0), ('mix', 1, 3), ('st', 2, 1), ('il', ('v', 3, 3)), ('st', 2, 2), ('mix', 2, 3), ('st', 2, 3), ('q', ('v', 3, 3)), ('mix', 3, 3), ('st', 3, 0), ('st', 3, 1), ('st', 3, 2), ('st', 3, 3)]
+KEYS_VEC = [2, 2, 1, 1, 0, 0, 0, 0]
+VAL_VEC = [4, 4, 2] + [0] * 13
 VAL_PE = []
-KEYS_PE = 8
+KEYS_PE = 0
 TURN = 2
 PLB = 8
 W_RATE = [2, 3, 4, 5, 6, 7, 8, 9, 10, 11, 12] + [12] * 13
@@ -339,7 +339,7 @@ def tile_smoothed_linear_slot_memory_d5_kernel(
 
         keys = [("k", gi, fi) for fi in range(FG) for gi in range(KG)]
         vals = [("v", gi, ci) for ci in range(len(CH)) for gi in range(FG)]
-        vec_planes = {k: KEYS_VEC for k in keys}
+        vec_planes = dict(zip(keys, KEYS_VEC))
         vec_planes.update(zip(vals, VAL_VEC))
         by_pe = set(keys[:KEYS_PE]) | {vals[n] for n in VAL_PE}
         for k in keys + vals:

@@ -25,8 +25,6 @@ TB = T // P
 ORDER = [('sw', ('k', 0, 0)), ('vw', ('k', 0, 0)), ('zt', 0), ('il', ('k', 0, 0)), ('ww', 0, 0, 0), ('zs', 0, 0), ('sw', ('k', 1, 0)), ('zt', 1), ('zs', 1, 0), ('ww', 0, 0, 1), ('vw', ('k', 1, 0)), ('sw', ('k', 0, 1)), ('zs', 0, 1), ('wt', 0, 0), ('zs', 1, 1), ('sw', ('k', 1, 1)), ('q', 'z', 0), ('q', 'z', 1), ('sw', ('k', 0, 2)), ('il', ('k', 1, 0)), ('vw', ('k', 0, 1)), ('q', ('k', 0, 0)), ('il', ('k', 0, 1)), ('sw', ('k', 1, 2)), ('vw', ('k', 1, 1)), ('q', ('k', 1, 0)), ('il', ('k', 1, 1)), ('sw', ('k', 0, 3)), ('sc', 0, 0), ('sc', 0, 1), ('q', ('k', 0, 1)), ('il', ('k', 0, 2)), ('sw', ('k', 1, 3)), ('q', ('k', 1, 1)), ('gate', 0, 0), ('gate', 0, 1), ('sc', 0, 2), ('ww', 0, 1, 0), ('il', ('k', 1, 2)), ('sc', 0, 3), ('wo', 0, 0), ('q', ('k', 0, 2)), ('gate', 0, 2), ('ww', 0, 1, 1), ('gate', 0, 3), ('sc', 1, 0), ('il', ('k', 0, 3)), ('sc', 1, 1), ('sw', ('v', 2, 0)), ('wt', 0, 1), ('ww', 1, 0, 0), ('q', 'h', 0), ('q', ('k', 1, 2)), ('gate', 1, 0), ('wo', 0, 1), ('gate', 1, 1), ('sc', 1, 2), ('il', ('k', 1, 3)), ('ww', 1, 0, 1), ('sc', 1, 3), ('ww', 1, 1, 0), ('vw', ('v', 0, 0)), ('wt', 1, 0), ('q', ('k', 0, 3)), ('ww', 1, 1, 1), ('gate', 1, 2), ('gate', 1, 3), ('sc', 2, 0), ('wo', 1, 0), ('il', ('v', 0, 0)), ('sc', 2, 1), ('sw', ('v', 3, 0)), ('wt', 1, 1), ('q', 'h', 1), ('vw', ('v', 1, 0)), ('wo', 1, 1), ('q', ('k', 1, 3)), ('gate', 2, 0), ('sw', ('v', 0, 1)), ('gate', 2, 1), ('sc', 2, 2), ('il', ('v', 1, 0)), ('sc', 2, 3), ('gate', 2, 2), ('sw', ('v', 1, 1)), ('gate', 2, 3), ('sc', 3, 0), ('q', 'w', 0, 0), ('sc', 3, 1), ('q', 'w', 1, 0), ('gate', 3, 0), ('dense', 0), ('sw', ('v', 2, 1)), ('gate', 3, 1), ('q', 'h', 2), ('vw', ('v', 2, 0)), ('q', ('v', 0, 0)), ('sc', 3, 2), ('ww', 2, 0, 0), ('il', ('v', 2, 0)), ('sc', 3, 3), ('mix', 0, 0), ('ww', 2, 0, 1), ('gate', 3, 2), ('gate', 3, 3), ('ww', 2, 1, 0), ('wt', 2, 0), ('q', ('v', 1, 0)), ('q', 'h', 3), ('mix', 1, 0), ('wo', 2, 0), ('q', 'w', 0, 1), ('q', 'w', 1, 1), ('ww', 2, 1, 1), ('il', ('v', 3, 0)), ('sw', ('v', 3, 1)), ('wt', 2, 1), ('q', ('v', 2, 0)), ('il', ('v', 0, 1)), ('mix', 2, 0), ('wo', 2, 1), ('q', ('v', 3, 0)), ('il', ('v', 1, 1)), ('mix', 3, 0), ('sw', ('v', 0, 2)), ('dense', 1), ('q', ('v', 0, 1)), ('st', 0, 0), ('il', ('v', 2, 1)), ('st', 0, 1), ('st', 0, 2), ('st', 0, 3), ('q', ('v', 1, 1)), ('mix', 0, 1), ('sw', ('v', 1, 2)), ('q', 'w', 0, 2), ('q', 'w', 1, 2), ('mix', 1, 1), ('sw', ('v', 2, 2)), ('il', ('v', 3, 1)), ('dense', 2), ('sw', ('v', 3, 2)), ('q', ('v', 2, 1)), ('il', ('v', 0, 2)), ('mix', 2, 1), ('sw', ('v', 0, 3)), ('q', ('v', 3, 1)), ('il', ('v', 1, 2)), ('mix', 3, 1), ('sw', ('v', 1, 3)), ('q', ('v', 0, 2)), ('il', ('v', 2, 2)), ('mix', 0, 2), ('st', 1, 0), ('q', ('v', 1, 2)), ('st', 1, 1), ('il', ('v', 3, 2)), ('mix', 1, 2), ('st', 1, 2), ('q', ('v', 2, 2)), ('il', ('v', 0, 3)), ('st', 1, 3), ('mix', 2, 2), ('sw', ('v', 2, 3)), ('q', ('v', 3, 2)), ('dense', 3), ('il', ('v', 1, 3)), ('q', ('v', 0, 3)), ('sw', ('v', 3, 3)), ('mix', 3, 2), ('il', ('v', 2, 3)), ('mix', 0, 3), ('q', ('v', 1, 3)), ('q', ('v', 2, 3)), ('st', 2, 0), ('mix', 1, 3), ('st', 2, 1), ('il', ('v', 3, 3)), ('st', 2, 2), ('mix', 2, 3), ('st', 2, 3), ('q', ('v', 3, 3)), ('mix', 3, 3), ('st', 3, 0), ('st', 3, 1), ('st', 3, 2), ('st', 3, 3)]
 KEYS_VEC = [2, 2, 1, 1, 0, 0, 0, 0]
 VAL_VEC = [4, 4, 2] + [0] * 13
-VAL_PE = []
-KEYS_PE = 0
 TURN = 2
 PLB = 8
 W_RATE = [2, 3, 4, 5, 6, 7, 8, 9, 10, 11, 12] + [12] * 13
@@ -54,16 +52,16 @@ def tile_smoothed_linear_slot_memory_d5_kernel(
         )
         ident = keep.tile([P, P], F32, name="ident")
         make_identity(nc, ident[:])
-        ident_bf = keep.tile([P, P], BF16, name="ident_bf")
-        nc.vector.tensor_copy(out=ident_bf[:], in_=ident[:])
-        g_sb = keep.tile([P, FG, 1, 4], BF16, name="g_sb")
-        nc.gpsimd.dma_start(
-            out=g_sb[:].rearrange("p g o t -> p g (o t)"), in_=g.rearrange("(g p t) -> p g t", p=P, t=4)
-        )
         ws = keep.tile([P, 96], F32, name="ws")
-        nc.gpsimd.dma_start(out=ws[:], in_=w_scale.rearrange("a b -> (a b)").partition_broadcast(P))
+        nc.scalar.dma_start(out=ws[:], in_=w_scale.rearrange("a b -> (a b)").partition_broadcast(P))
+        g_sb = keep.tile([P, FG, 1, 4], BF16, name="g_sb")
         vs = keep.tile([P, FG, 4], F32, name="vs")
-        nc.gpsimd.dma_start(out=vs[:], in_=values_scale.rearrange("(g p t) o -> p g (t o)", p=P, t=4))
+
+        def load_late():
+            nc.sync.dma_start(
+                out=g_sb[:].rearrange("p g o t -> p g (o t)"), in_=g.rearrange("(g p t) -> p g t", p=P, t=4)
+            )
+            nc.sync.dma_start(out=vs[:], in_=values_scale.rearrange("(g p t) o -> p g (t o)", p=P, t=4))
 
         key_rows = keys_bytes.rearrange("(g p t) n -> g p t n", p=P, t=4)
         val_rows = values_bytes.rearrange("(g p t) n -> g p t n", p=P, t=4)
@@ -94,6 +92,7 @@ def tile_smoothed_linear_slot_memory_d5_kernel(
         load_keys(1, 0, 512)
         load_x(1)
         load_w(0, 1)
+        load_late()
         load_keys(0, 512, 512)
         load_keys(1, 512, 512)
         load_w(1, 0)
@@ -222,38 +221,12 @@ def tile_smoothed_linear_slot_memory_d5_kernel(
             pl = planes.pop(key)
             if key[0] == "k":
                 nc.vector.tensor_copy(
-                    out=gr[:].rearrange("p (t m) j -> p t m j", t=4), in_=pl[:].rearrange("p j (m t) -> p t m j", t=4)
+                    out=gr[:].rearrange("p (t m) j -> p m j t", t=4), in_=pl[:].rearrange("p j (m t) -> p m j t", t=4)
                 )
             else:
                 nc.vector.tensor_copy(
                     out=gr[:].rearrange("p (n i) j -> p n j i", i=4), in_=pl[:].rearrange("p j (n i) -> p n j i", i=4)
                 )
-
-        def pe_interleave(key, half):
-            pl = planes[key]
-            bank = psum.tile([P, 1024], BF16, name="turn", bufs=TURN)
-            for q in range(2):
-                t = 2 * half + q
-                if key[0] == "k":
-                    rhs = pl[:].rearrange("p j (m t) -> p t m j", t=4)[:, t]
-                else:
-                    rhs = pl[:, :, P * t : P * t + P].rearrange("p j n -> p n j")
-                nc.tensor.matmul(
-                    out=bank[:, 512 * q : 512 * q + 512].rearrange("p (n j) -> p n j", j=4),
-                    lhsT=ident_bf[:],
-                    rhs=rhs,
-                    start=True,
-                    stop=True,
-                )
-            banks[key, half] = bank
-            if half == 1:
-                planes.pop(key)
-
-        def pe_copy(key, half):
-            gr = get(grouped, key, lambda: grouped_tile("gr", 3))
-            nc.scalar.copy(
-                out=gr[:, 256 * half : 256 * half + 256, :].rearrange("p n j -> p (n j)"), in_=banks.pop((key, half))[:]
-            )
 
         def w_widen(ci, h, i):
             t = get(wb, (ci, h), lambda: stage.tile([P, 2, D], BF16, name="wb", bufs=2))
@@ -341,11 +314,6 @@ def tile_smoothed_linear_slot_memory_d5_kernel(
         vals = [("v", gi, ci) for ci in range(len(CH)) for gi in range(FG)]
         vec_planes = dict(zip(keys, KEYS_VEC))
         vec_planes.update(zip(vals, VAL_VEC))
-        by_pe = set(keys[:KEYS_PE]) | {vals[n] for n in VAL_PE}
-        for k in keys + vals:
-            if k in by_pe and k not in vals:
-                pass
-
         def v_widen(k):
             if vec_planes[k]:
                 job("V", ("vw", k), [], lambda: widen(k, range(vec_planes[k]), True))
@@ -354,13 +322,11 @@ def tile_smoothed_linear_slot_memory_d5_kernel(
             return ([("vw", k)] if vec_planes[k] else []) + ([("sw", k)] if vec_planes[k] < 4 else [])
 
         def v_inter(k):
-            if k not in by_pe:
-                job("V", ("il", k), widened(k), lambda: interleave(k))
+            job("V", ("il", k), widened(k), lambda: interleave(k))
 
         def v_quant(k):
             dst = kq[k[1:]] if k[0] == "k" else vq[k[1:]]
-            deps = [("pc", k, 0), ("pc", k, 1)] if k in by_pe else [("il", k)]
-            job("V", ("q", k), deps, lambda: quantize(dst, grouped[k]))
+            job("V", ("q", k), [("il", k)], lambda: quantize(dst, grouped[k]))
 
         def v_wquant(ci):
             for gi in range(KG):
@@ -425,11 +391,6 @@ def tile_smoothed_linear_slot_memory_d5_kernel(
             if vec_planes[k] < 4:
                 job("S", ("sw", k), [], lambda: widen(k, range(vec_planes[k], 4), False))
 
-        def s_copy(k):
-            for half in range(2):
-                if k in by_pe:
-                    job("S", ("pc", k, half), [("pe", k, half)], lambda half=half: pe_copy(k, half))
-
         def s_w(n, i):
             if n < len(halves):
                 job("S", ("ww",) + halves[n] + (i,), [], lambda: w_widen(*halves[n], i))
@@ -453,12 +414,10 @@ def tile_smoothed_linear_slot_memory_d5_kernel(
 
         for r, k in enumerate(keys):
             s_widen(k)
-            s_copy(k)
             s_wtiles(W_RATE[r])
         for n in range(len(vals)):
             if n < len(vals):
                 s_widen(vals[n])
-                s_copy(vals[n])
                 s_wtiles(W_RATE[8 + n])
             ci = (n - ST_LAG) // 4
             if (n - ST_LAG) % 4 == 0 and 0 <= ci < 3:
@@ -470,11 +429,6 @@ def tile_smoothed_linear_slot_memory_d5_kernel(
                 if ("st", ci, i) not in jobs:
                     e = "V" if ci == last and i % 2 else "S"
                     job(e, ("st", ci, i), [("mix", 3, ci)], lambda ci=ci, i=i, e=e: store(ci, i, e == "V"))
-
-        def t_pe(k):
-            for half in range(2):
-                if k in by_pe:
-                    job("T", ("pe", k, half), widened(k), lambda half=half: pe_interleave(k, half))
 
         def t_scores(fi):
             for i in range(TB):
@@ -488,21 +442,15 @@ def tile_smoothed_linear_slot_memory_d5_kernel(
                 job("T", ("wt",) + halves[n], [("ww",) + halves[n] + (i,) for i in range(2)], lambda: w_turn(*halves[n]))
 
         t_zturn(0)
-        t_pe(keys[0])
         t_zturn(1)
         t_wturn(0)
-        t_pe(keys[1])
         for r, k in enumerate(keys):
-            if r + 2 < len(keys):
-                t_pe(keys[r + 2])
             if r % 2 == 1:
                 t_scores(r // 2)
             t_wturn(r + 1)
         for ci in range(len(CH)):
             job("T", ("dense", ci), [("q", "w", gi, min(ci, 2)) for gi in range(KG)] + [("st", ci - 2, i) for i in range(TB) if ci > 1] + ([("wt", 2, 1), ("gate", 3, 3)] if ci == 1 else []), lambda ci=ci: dense(ci))
             for gi in range(FG):
-                if 4 * ci + gi + 1 < len(vals):
-                    t_pe(vals[4 * ci + gi + 1])
                 job("T", ("mix", gi, ci), [("q", "h", gi), ("q", ("v", gi, ci)), ("mix", gi - 1, ci) if gi else ("dense", ci)], lambda gi=gi, ci=ci: mix(gi, ci))
 
         for key in ORDER:

from contextlib import ExitStack

import concourse.mybir as mybir
from concourse.masks import make_identity

T, D, F, N = 512, 1024, 2048, 1536
P = 128
FLOPS = 2 * T * (D * N + D * F + F * N)

F32 = mybir.dt.float32
BF16 = mybir.dt.bfloat16
U32 = mybir.dt.uint32
U8 = mybir.dt.uint8
FP8 = mybir.dt.float8_e4m3fn
FP8X4 = mybir.dt.float8_e4m3fn_x4
MULT = mybir.AluOpType.mult
MAX = mybir.AluOpType.max
COPY = mybir.ActivationFunctionType.Copy

KG = D // 512
FG = F // 512
NC = N // 512
TB = T // P

ORDER = [('sw', ('k', 0, 0)), ('vw', ('k', 0, 0)), ('zt', 0), ('il', ('k', 0, 0)), ('ww', 0, 0, 0), ('zs', 0, 0), ('sw', ('k', 1, 0)), ('zt', 1), ('zs', 1, 0), ('ww', 0, 0, 1), ('vw', ('k', 1, 0)), ('sw', ('k', 0, 1)), ('zs', 0, 1), ('wt', 0, 0), ('zs', 1, 1), ('sw', ('k', 1, 1)), ('q', 'z', 0), ('q', 'z', 1), ('sw', ('k', 0, 2)), ('il', ('k', 1, 0)), ('vw', ('k', 0, 1)), ('q', ('k', 0, 0)), ('il', ('k', 0, 1)), ('sw', ('k', 1, 2)), ('vw', ('k', 1, 1)), ('q', ('k', 1, 0)), ('il', ('k', 1, 1)), ('sw', ('k', 0, 3)), ('sc', 0, 0), ('sc', 0, 1), ('q', ('k', 0, 1)), ('il', ('k', 0, 2)), ('sw', ('k', 1, 3)), ('q', ('k', 1, 1)), ('gate', 0, 0), ('gate', 0, 1), ('sc', 0, 2), ('ww', 0, 1, 0), ('il', ('k', 1, 2)), ('sc', 0, 3), ('wo', 0, 0), ('q', ('k', 0, 2)), ('gate', 0, 2), ('ww', 0, 1, 1), ('gate', 0, 3), ('sc', 1, 0), ('il', ('k', 0, 3)), ('sc', 1, 1), ('sw', ('v', 2, 0)), ('wt', 0, 1), ('ww', 1, 0, 0), ('q', 'h', 0), ('q', ('k', 1, 2)), ('gate', 1, 0), ('wo', 0, 1), ('gate', 1, 1), ('sc', 1, 2), ('il', ('k', 1, 3)), ('ww', 1, 0, 1), ('sc', 1, 3), ('ww', 1, 1, 0), ('vw', ('v', 0, 0)), ('wt', 1, 0), ('q', ('k', 0, 3)), ('ww', 1, 1, 1), ('gate', 1, 2), ('gate', 1, 3), ('sc', 2, 0), ('wo', 1, 0), ('il', ('v', 0, 0)), ('sc', 2, 1), ('sw', ('v', 3, 0)), ('wt', 1, 1), ('q', 'h', 1), ('vw', ('v', 1, 0)), ('wo', 1, 1), ('q', ('k', 1, 3)), ('gate', 2, 0), ('sw', ('v', 0, 1)), ('gate', 2, 1), ('sc', 2, 2), ('il', ('v', 1, 0)), ('sc', 2, 3), ('gate', 2, 2), ('sw', ('v', 1, 1)), ('gate', 2, 3), ('sc', 3, 0), ('q', 'w', 0, 0), ('sc', 3, 1), ('q', 'w', 1, 0), ('gate', 3, 0), ('dense', 0), ('sw', ('v', 2, 1)), ('gate', 3, 1), ('q', 'h', 2), ('vw', ('v', 2, 0)), ('q', ('v', 0, 0)), ('sc', 3, 2), ('ww', 2, 0, 0), ('il', ('v', 2, 0)), ('sc', 3, 3), ('mix', 0, 0), ('ww', 2, 0, 1), ('gate', 3, 2), ('gate', 3, 3), ('ww', 2, 1, 0), ('wt', 2, 0), ('q', ('v', 1, 0)), ('q', 'h', 3), ('mix', 1, 0), ('wo', 2, 0), ('q', 'w', 0, 1), ('q', 'w', 1, 1), ('ww', 2, 1, 1), ('il', ('v', 3, 0)), ('sw', ('v', 3, 1)), ('wt', 2, 1), ('q', ('v', 2, 0)), ('il', ('v', 0, 1)), ('mix', 2, 0), ('wo', 2, 1), ('q', ('v', 3, 0)), ('il', ('v', 1, 1)), ('mix', 3, 0), ('sw', ('v', 0, 2)), ('dense', 1), ('q', ('v', 0, 1)), ('st', 0, 0), ('il', ('v', 2, 1)), ('st', 0, 1), ('st', 0, 2), ('st', 0, 3), ('q', ('v', 1, 1)), ('mix', 0, 1), ('sw', ('v', 1, 2)), ('q', 'w', 0, 2), ('q', 'w', 1, 2), ('mix', 1, 1), ('sw', ('v', 2, 2)), ('il', ('v', 3, 1)), ('dense', 2), ('sw', ('v', 3, 2)), ('q', ('v', 2, 1)), ('il', ('v', 0, 2)), ('mix', 2, 1), ('sw', ('v', 0, 3)), ('q', ('v', 3, 1)), ('il', ('v', 1, 2)), ('mix', 3, 1), ('sw', ('v', 1, 3)), ('q', ('v', 0, 2)), ('il', ('v', 2, 2)), ('mix', 0, 2), ('st', 1, 0), ('q', ('v', 1, 2)), ('st', 1, 1), ('il', ('v', 3, 2)), ('mix', 1, 2), ('st', 1, 2), ('q', ('v', 2, 2)), ('il', ('v', 0, 3)), ('st', 1, 3), ('mix', 2, 2), ('sw', ('v', 2, 3)), ('q', ('v', 3, 2)), ('dense', 3), ('il', ('v', 1, 3)), ('q', ('v', 0, 3)), ('sw', ('v', 3, 3)), ('mix', 3, 2), ('il', ('v', 2, 3)), ('mix', 0, 3), ('q', ('v', 1, 3)), ('q', ('v', 2, 3)), ('st', 2, 0), ('mix', 1, 3), ('st', 2, 1), ('il', ('v', 3, 3)), ('st', 2, 2), ('mix', 2, 3), ('st', 2, 3), ('q', ('v', 3, 3)), ('mix', 3, 3), ('st', 3, 0), ('st', 3, 1), ('st', 3, 2), ('st', 3, 3)]
KEYS_VEC = [2, 2, 1, 1, 0, 0, 0, 0]
VAL_VEC = [4, 4, 2] + [0] * 13
TURN = 2
PLB = 8
W_RATE = [2, 3, 4, 5, 6, 7, 8, 9, 10, 11, 12] + [12] * 13
ST_LAG = 7
GATE_LAG = 3
SC = 2
CH = [(0, 512), (512, 512), (1024, 256), (1280, 256)]


def tile_smoothed_linear_slot_memory_d5_kernel(
    tc, x, c, g, w_bytes, w_scale, keys_bytes, keys_scale, values_bytes, values_scale, out
):
    nc = tc.nc
    with ExitStack() as ctx:
        keep = ctx.enter_context(tc.tile_pool(name="keep", bufs=1))
        stage = ctx.enter_context(tc.tile_pool(name="stage", bufs=4))
        psum = ctx.enter_context(tc.psum_pool(name="psum", bufs=1))
        ctx.enter_context(tc.manual_schedule())

        ks = keep.tile([P, KG, 4], F32, name="ks")
        nc.sync.dma_start(out=ks[:], in_=keys_scale.rearrange("(g p t) o -> p g (t o)", p=P, t=4))
        c_sb = keep.tile([P, KG, 1, 2, 2], BF16, name="c_sb")
        nc.scalar.dma_start(
            out=c_sb[:].rearrange("p g o u e -> p g (o u e)"), in_=c.rearrange("(g p t) -> p g t", p=P, t=4)
        )
        ident = keep.tile([P, P], F32, name="ident")
        make_identity(nc, ident[:])
        ws = keep.tile([P, 96], F32, name="ws")
        nc.scalar.dma_start(out=ws[:], in_=w_scale.rearrange("a b -> (a b)").partition_broadcast(P))
        g_sb = keep.tile([P, FG, 1, 4], BF16, name="g_sb")
        vs = keep.tile([P, FG, 4], F32, name="vs")

        def load_late():
            nc.sync.dma_start(
                out=g_sb[:].rearrange("p g o t -> p g (o t)"), in_=g.rearrange("(g p t) -> p g t", p=P, t=4)
            )
            nc.sync.dma_start(out=vs[:], in_=values_scale.rearrange("(g p t) o -> p g (t o)", p=P, t=4))

        key_rows = keys_bytes.rearrange("(g p t) n -> g p t n", p=P, t=4)
        val_rows = values_bytes.rearrange("(g p t) n -> g p t n", p=P, t=4)
        w_rows = w_bytes.rearrange("(b p) k -> p b k", p=P)
        x_rows = x.rearrange("(i p) k -> p i k", p=P)

        kraw, vraw, wraw, xt = {}, {}, {}, {}

        def load_keys(gi, lo, width):
            raw = keep.tile([P, 4, width], U8, name="kraw%d_%d" % (gi, lo))
            nc.sync.dma_start(out=raw[:], in_=key_rows[gi][:, :, lo : lo + width])
            for f0 in range(lo, lo + width, 512):
                kraw[gi, f0 // 512] = (raw, f0 - lo)

        def load_x(h):
            xs = keep.tile([P, 2, D], BF16, name="x%d" % h)
            nc.sync.dma_start(out=xs[:], in_=x_rows[:, 2 * h : 2 * h + 2, :])
            xt[h] = xs

        def load_w(ci, h):
            raw = keep.tile([P, 2, D], U8, name="wraw%d_%d" % (ci, h))
            nc.sync.dma_start(out=raw[:], in_=w_rows[:, 4 * ci + 2 * h : 4 * ci + 2 * h + 2, :])
            wraw[ci, h] = raw

        load_keys(0, 0, 512)
        load_x(0)
        load_w(0, 0)
        load_keys(1, 0, 512)
        load_x(1)
        load_w(0, 1)
        load_late()
        load_keys(0, 512, 512)
        load_keys(1, 512, 512)
        load_w(1, 0)
        load_keys(0, 1024, 1024)
        load_w(1, 1)
        load_keys(1, 1024, 1024)
        load_w(2, 0)
        load_w(2, 1)
        for ci in range(NC):
            for gi in range(FG):
                raw = keep.tile([P, 4, 512], U8, name="vraw%d_%d" % (gi, ci))
                nc.sync.dma_start(out=raw[:], in_=val_rows[gi][:, :, 512 * ci : 512 * ci + 512])
                vraw[gi, ci] = raw

        rc = keep.tile([P, KG, 1, 2, 2], F32, name="rc")
        nc.vector.reciprocal(out=rc[:], in_=c_sb[:])

        def operand(name, width=512):
            return (
                keep.tile([P, width], U32, name=name + "_q", align_bytes=64),
                keep.tile([P, width], U8, name=name + "_s", align_bytes=64),
            )

        zq = [operand("z%d" % gi) for gi in range(KG)]
        kq = {(gi, fi): operand("k%d_%d" % (gi, fi)) for gi in range(KG) for fi in range(FG)}
        wq = {(gi, ci): operand("w%d_%d" % (gi, ci)) for gi in range(KG) for ci in range(NC)}
        hq = [operand("h%d" % gi) for gi in range(FG)]
        vq = {(gi, ci): operand("v%d_%d" % (gi, ci), CH[ci][1]) for gi in range(FG) for ci in range(len(CH))}

        def quantize(dst, src):
            nc.vector.quantize_mx(
                out=dst[0][:].bitcast(FP8X4), scales=dst[1][:], in_=src[:].rearrange("p n j -> p (n j)")
            )

        def grouped_tile(name, bufs, width=512):
            return stage.tile([P, width, 4], BF16, name=name, bufs=bufs, align_bytes=64)

        def mm(o, a, a_lo, b, b_lo, width, start, stop):
            nc.tensor.matmul_mx(
                out=o,
                lhsT=a[0][:, a_lo : a_lo + P].bitcast(FP8X4),
                lhsT_scale=a[1][:, a_lo : a_lo + P],
                rhs=b[0][:, b_lo : b_lo + width].bitcast(FP8X4),
                rhs_scale=b[1][:, b_lo : b_lo + width],
                start=start,
                stop=stop,
            )

        zg = [grouped_tile("wg%d" % gi, 2) for gi in range(KG)]

        def z_turn(gi, h):
            bank = psum.tile([P, 2, 256], F32, name="o%d" % (2 * h + gi), bufs=1)
            for i in range(2):
                words = xt[h][:, i, :].bitcast(F32)
                for u in range(2):
                    nc.tensor.transpose(
                        bank[:, u, P * i : P * i + P], words[:, 256 * gi + u : 256 * (gi + 1) : 2], ident[:]
                    )
            return bank

        def z_scale(gi, h, bank):
            nc.vector.tensor_tensor(
                out=zg[gi][:, 256 * h : 256 * h + 256, :].rearrange("p r (u e) -> p r u e", u=2),
                in0=bank[:].rearrange("p u r -> p (u r)").bitcast(BF16).rearrange("p (u r e) -> p r u e", u=2, e=2),
                in1=rc[:, gi].to_broadcast([P, 256, 2, 2]),
                op=MULT,
            )

        jobs, lists = {}, {"V": [], "S": [], "T": []}

        def job(engine, key, deps, fn):
            jobs[key] = (engine, deps, fn)
            lists[engine].append(key)

        done, cursor, active = set(), {"V": 0, "S": 0, "T": 0}, []

        def emit(key):
            if key in done:
                return
            engine = jobs[key][0]
            while key not in done:
                k = lists[engine][cursor[engine]]
                assert k not in active, (k, active)
                active.append(k)
                for d in jobs[k][1]:
                    emit(d)
                active.pop()
                if k in done:
                    continue
                cursor[engine] += 1
                done.add(k)
                jobs[k][2]()

        planes, grouped, banks, wb, obank = {}, {}, {}, {}, {}

        def get(d, key, make):
            if key not in d:
                d[key] = make()
            return d[key]

        def source(key):
            kind, gi, ni = key
            if kind == "k":
                raw, lo = kraw[gi, ni]
                return raw, lo, ks[:, gi, :]
            return vraw[gi, CH[ni][0] // 512], CH[ni][0] % 512, vs[:, gi, :]

        def width_of(key):
            return 512 if key[0] == "k" else CH[key[2]][1]

        def widen(key, js, vec):
            raw, lo, scale = source(key)
            w = width_of(key)
            pl = get(planes, key, lambda: stage.tile([P, 4, w], BF16, name="planes", bufs=PLB))
            for j in js:
                src = raw[:, j, lo : lo + w].bitcast(FP8)
                if vec:
                    nc.vector.tensor_scalar(
                        out=pl[:, j, :], in0=src, scalar1=scale[:, j : j + 1], scalar2=None, op0=MULT
                    )
                else:
                    nc.scalar.activation(out=pl[:, j, :], in_=src, func=COPY, scale=scale[:, j : j + 1])

        def interleave(key):
            gr = get(grouped, key, lambda: grouped_tile("gr", 3, width_of(key)))
            pl = planes.pop(key)
            if key[0] == "k":
                nc.vector.tensor_copy(
                    out=gr[:].rearrange("p (t m) j -> p m j t", t=4), in_=pl[:].rearrange("p j (m t) -> p m j t", t=4)
                )
            else:
                nc.vector.tensor_copy(
                    out=gr[:].rearrange("p (n i) j -> p n j i", i=4), in_=pl[:].rearrange("p j (n i) -> p n j i", i=4)
                )

        def w_widen(ci, h, i):
            t = get(wb, (ci, h), lambda: stage.tile([P, 2, D], BF16, name="wb", bufs=2))
            b = 4 * ci + 2 * h + i
            for q in range(8):
                nc.scalar.activation(
                    out=t[:, i, P * q : P * q + P],
                    in_=wraw[ci, h][:, i, P * q : P * q + P].bitcast(FP8),
                    func=COPY,
                    scale=ws[:, 8 * b + q : 8 * b + q + 1],
                )

        def w_turn(ci, h):
            for gi in range(KG):
                if ci < 2:
                    bank = psum.tile([P, 2, 256], F32, name="o%d" % (2 * h + gi), bufs=1)
                else:
                    bank = psum.tile([P, 2, 256], F32, name="turn", bufs=TURN)
                for i in range(2):
                    words = wb[ci, h][:, i, :].bitcast(F32)
                    for u in range(2):
                        nc.tensor.transpose(
                            bank[:, u, P * i : P * i + P], words[:, 256 * gi + u : 256 * (gi + 1) : 2], ident[:]
                        )
                banks["w", ci, h, gi] = bank

        def w_out(ci, h):
            for gi in range(KG):
                gr = get(grouped, ("w", gi, ci), lambda: grouped_tile("wg%d" % gi, 2))
                dst = gr[:].rearrange("p n j -> p (n j)").bitcast(F32)
                nc.scalar.copy(
                    out=dst[:, 512 * h : 512 * h + 512].rearrange("p (n u) -> p n u", u=2),
                    in_=banks.pop(("w", ci, h, gi))[:].rearrange("p u n -> p n u"),
                )

        def z_turns(h):
            for gi in range(KG):
                banks["z", gi, h] = z_turn(gi, h)

        def scores(fi, i):
            bank = psum.tile([P, 4, P], F32, name="sc", bufs=SC)
            for t in range(4):
                for gi in range(KG):
                    mm(bank[:, t, :], kq[gi, fi], P * t, zq[gi], P * i, P, gi == 0, gi == KG - 1)
            banks["s", fi, i] = bank

        def gate(fi, i):
            gr = get(grouped, ("h", fi), lambda: grouped_tile("hg", 2))
            nc.vector.scalar_tensor_tensor(
                out=gr[:, P * i : P * i + P, :],
                in0=banks.pop(("s", fi, i))[:].rearrange("p t n -> p n t"),
                scalar=0.0,
                in1=g_sb[:, fi].to_broadcast([P, P, 4]),
                op0=MAX,
                op1=MULT,
            )

        def dense(ci):
            lo, width = CH[ci]
            for i in range(TB):
                if ci % 2 == 0:
                    obank[ci, i] = psum.tile([P, width], F32, name="o%d" % i, bufs=1)
                elif i < 2:
                    obank[ci, i] = psum.tile([P, width], F32, name="sc", bufs=SC)
                else:
                    obank[ci, i] = psum.tile([P, width], F32, name="turn", bufs=TURN)
            for gi in range(KG):
                for i in range(TB):
                    mm(obank[ci, i][:], zq[gi], P * i, wq[gi, lo // 512], lo % 512, width, gi == 0, False)

        def mix(gi, ci):
            for i in range(TB):
                mm(obank[ci, i][:], hq[gi], P * i, vq[gi, ci], 0, CH[ci][1], False, gi == FG - 1)

        def store(ci, i, vec):
            lo, width = CH[ci]
            res = stage.tile([P, width], F32, name="res", bufs=8)
            if vec:
                nc.vector.tensor_copy(out=res[:], in_=obank[ci, i][:])
            else:
                nc.scalar.copy(out=res[:], in_=obank[ci, i][:])
            nc.sync.dma_start(out=out[P * i : P * i + P, lo : lo + width], in_=res[:])

        keys = [("k", gi, fi) for fi in range(FG) for gi in range(KG)]
        vals = [("v", gi, ci) for ci in range(len(CH)) for gi in range(FG)]
        vec_planes = dict(zip(keys, KEYS_VEC))
        vec_planes.update(zip(vals, VAL_VEC))
        def v_widen(k):
            if vec_planes[k]:
                job("V", ("vw", k), [], lambda: widen(k, range(vec_planes[k]), True))

        def widened(k):
            return ([("vw", k)] if vec_planes[k] else []) + ([("sw", k)] if vec_planes[k] < 4 else [])

        def v_inter(k):
            job("V", ("il", k), widened(k), lambda: interleave(k))

        def v_quant(k):
            dst = kq[k[1:]] if k[0] == "k" else vq[k[1:]]
            job("V", ("q", k), [("il", k)], lambda: quantize(dst, grouped[k]))

        def v_wquant(ci):
            for gi in range(KG):
                job(
                    "V",
                    ("q", "w", gi, ci),
                    [("wo", ci, 0), ("wo", ci, 1)],
                    lambda gi=gi: quantize(wq[gi, ci], grouped["w", gi, ci]),
                )

        def v_gates(fi, blocks):
            for i in blocks:
                job("V", ("gate", fi, i), [("sc", fi, i)], lambda i=i: gate(fi, i))

        def v_hquant(fi):
            job("V", ("q", "h", fi), [("gate", fi, i) for i in range(TB)], lambda: quantize(hq[fi], grouped["h", fi]))

        def v_z(h):
            for gi in range(KG):
                job("V", ("zs", gi, h), [("zt", h)], lambda gi=gi: z_scale(gi, h, banks.pop(("z", gi, h))))

        v_widen(keys[0])
        v_z(0)
        v_widen(keys[1])
        v_inter(keys[0])
        v_z(1)
        for gi in range(KG):
            job("V", ("q", "z", gi), [("zs", gi, 0), ("zs", gi, 1)], lambda gi=gi: quantize(zq[gi], zg[gi]))
        v_inter(keys[1])
        for r, k in enumerate(keys):
            ahead = (keys + vals)[r + 2]
            v_widen(ahead)
            v_quant(k)
            if r >= GATE_LAG:
                s = r - GATE_LAG
                v_gates(s // 2, (0, 1) if s % 2 == 0 else (2, 3))
            v_inter(ahead)
            if r > GATE_LAG and (r - GATE_LAG) % 2 == 1:
                v_hquant((r - GATE_LAG) // 2)
        for s in range(8 - GATE_LAG, 8):
            v_gates(s // 2, (0, 1) if s % 2 == 0 else (2, 3))
            if s == 8 - GATE_LAG:
                v_wquant(0)
            if s == 6:
                v_hquant(2)
        for n, k in enumerate(vals):
            if n + 2 < len(vals):
                v_widen(vals[n + 2])
            if n + 1 < len(vals) and n > 0:
                v_inter(vals[n + 1])
            if n == 0:
                v_hquant(3)
            v_quant(k)
            if n == 1:
                v_wquant(1)
            if n == 5:
                v_wquant(2)

        halves = [(ci, h) for ci in range(NC) for h in range(2)]

        def s_widen(k):
            if vec_planes[k] < 4:
                job("S", ("sw", k), [], lambda: widen(k, range(vec_planes[k], 4), False))

        def s_w(n, i):
            if n < len(halves):
                job("S", ("ww",) + halves[n] + (i,), [], lambda: w_widen(*halves[n], i))

        def s_wout(n):
            if 0 <= n < len(halves):
                job("S", ("wo",) + halves[n], [("wt",) + halves[n]], lambda: w_out(*halves[n]))

        tiles = [(n, i) for n in range(len(halves)) for i in range(2)]
        w_next = [0]

        def s_wtiles(upto):
            while w_next[0] < min(upto, 12):
                n, i = tiles[w_next[0]]
                s_w(n, i)
                w_next[0] += 1
                if i == 0:
                    s_wout(n - 1)
                if w_next[0] == 12:
                    s_wout(n)

        for r, k in enumerate(keys):
            s_widen(k)
            s_wtiles(W_RATE[r])
        for n in range(len(vals)):
            if n < len(vals):
                s_widen(vals[n])
                s_wtiles(W_RATE[8 + n])
            ci = (n - ST_LAG) // 4
            if (n - ST_LAG) % 4 == 0 and 0 <= ci < 3:
                for i in range(TB):
                    job("S", ("st", ci, i), [("mix", 3, ci)], lambda ci=ci, i=i: store(ci, i, False))
        last = len(CH) - 1
        for ci in range(1, last + 1):
            for i in range(TB):
                if ("st", ci, i) not in jobs:
                    e = "V" if ci == last and i % 2 else "S"
                    job(e, ("st", ci, i), [("mix", 3, ci)], lambda ci=ci, i=i, e=e: store(ci, i, e == "V"))

        def t_scores(fi):
            for i in range(TB):
                job("T", ("sc", fi, i), [("q", ("k", gi, fi)) for gi in range(KG)] + [("q", "z", gi) for gi in range(KG)], lambda i=i: scores(fi, i))

        def t_zturn(h):
            job("T", ("zt", h), [], lambda: z_turns(h))

        def t_wturn(n):
            if 0 <= n < len(halves):
                job("T", ("wt",) + halves[n], [("ww",) + halves[n] + (i,) for i in range(2)], lambda: w_turn(*halves[n]))

        t_zturn(0)
        t_zturn(1)
        t_wturn(0)
        for r, k in enumerate(keys):
            if r % 2 == 1:
                t_scores(r // 2)
            t_wturn(r + 1)
        for ci in range(len(CH)):
            job("T", ("dense", ci), [("q", "w", gi, min(ci, 2)) for gi in range(KG)] + [("st", ci - 2, i) for i in range(TB) if ci > 1] + ([("wt", 2, 1), ("gate", 3, 3)] if ci == 1 else []), lambda ci=ci: dense(ci))
            for gi in range(FG):
                job("T", ("mix", gi, ci), [("q", "h", gi), ("q", ("v", gi, ci)), ("mix", gi - 1, ci) if gi else ("dense", ci)], lambda gi=gi, ci=ci: mix(gi, ci))

        for key in ORDER:
            jobs[key][2]()
